import numpy as np
import ml_dtypes


def mxq(x, axis, fmt="e4m3"):
    dtype, down = {"e4m3": (ml_dtypes.float8_e4m3fn, 7), "e5m2": (ml_dtypes.float8_e5m2, 14)}[fmt]
    v = np.moveaxis(np.asarray(x, np.float32).astype(ml_dtypes.bfloat16).astype(np.float64), axis, -1)
    blocks = v.reshape(v.shape[:-1] + (-1, 32))
    amax = np.abs(blocks).max(-1, keepdims=True)
    byte = np.maximum(np.where(amax > 0, np.frexp(amax)[1] - 1 + 127, 0) - down, 1)
    scale = np.exp2(byte - 127.0)
    codes = (blocks / scale).astype(np.float32).astype(dtype).astype(np.float64)
    return np.moveaxis((codes * scale).reshape(v.shape), -1, axis)


WIDE = False


def mx_kscale(k):
    if not WIDE:
        return np.ones(k)
    levels = np.array([10, -10, 5, -5, 0])
    if k % 512:
        return np.exp2(np.random.permutation(np.resize(levels, k // 32))).repeat(32)
    a = np.empty((k // 512, 16))
    for p in range(k // 512):
        a[p, :8] = np.random.permutation(np.resize(levels, 8))
        for g in range(8):
            far = levels[np.abs(levels - a[p, g]) >= 10]
            a[p, g + 8] = far[np.random.randint(len(far))]
    return np.exp2(a.ravel()).repeat(32)


BF16 = ml_dtypes.bfloat16


def bf(x):
    return np.asarray(x, np.float32).astype(BF16)


def f64(x):
    return np.asarray(x).astype(np.float64)


E2M1 = np.array([0.0, 0.5, 1.0, 1.5, 2.0, 3.0, 4.0, 6.0, -0.0, -0.5, -1.0, -1.5, -2.0, -3.0, -4.0, -6.0])


def pack_weight(w, fmt):
    k, n = w.shape
    w = f64(bf(w)).reshape(k // 32, 32, n)
    amax = np.abs(w).max(1)
    if fmt == "e4m3":
        byte = np.frexp(amax)[1] - 1 + 127 - 7
    else:
        mant, ex = np.frexp(amax / 6.0)
        byte = np.where(mant > 0.5, ex, ex - 1) + 127
    byte = np.clip(np.where(amax > 0, byte, 1), 1, 254)
    scaled = (w * np.exp2(127.0 - byte)[:, None, :]).reshape(k, n).astype(np.float32)
    by_word = np.ascontiguousarray(scaled.reshape(k // 512, 128, 4, n).transpose(0, 1, 3, 2))
    if fmt == "e4m3":
        words = by_word.astype(ml_dtypes.float8_e4m3fn).view(np.uint8)
    else:
        c = by_word.astype(ml_dtypes.float4_e2m1fn).view(np.uint8) & 0xF
        words = c[..., 0::2] | (c[..., 1::2] << 4)
    return np.ascontiguousarray(words), np.ascontiguousarray(byte.astype(np.uint8).reshape(k // 512, 16, n))


def unpack_weight(words, scales, fmt):
    g, p, n, _ = words.shape
    if fmt == "e4m3":
        vals = np.ascontiguousarray(words).view(ml_dtypes.float8_e4m3fn).astype(np.float64)
    else:
        nib = np.empty((g, p, n, 4), np.uint8)
        nib[..., 0::2] = words & 0xF
        nib[..., 1::2] = words >> 4
        vals = E2M1[nib]
    vals = vals * np.repeat(np.exp2(scales.astype(np.float64) - 127.0), 8, axis=1)[..., None]
    return vals.transpose(0, 1, 3, 2).reshape(g * 512, n)
def pack4(w):
    words, scales = pack_weight(w, "e2m1")
    return words.reshape(words.shape[0], 128, -1), scales


def unpack4(words, scales):
    return unpack_weight(words.reshape(words.shape[0], 128, -1, 2), scales, "e2m1")


def planes(Y):
    n, m = Y.shape
    b = f64(bf(Y)).reshape(n // 32, 32, m)
    amax = np.abs(b).max(1)
    byte = np.clip(np.where(amax > 0, np.frexp(amax)[1] - 1 + 127 - 7, 1), 1, 254)
    codes = (b * np.exp2(127.0 - byte)[:, None, :]).reshape(n, m).astype(np.float32).astype(ml_dtypes.float8_e4m3fn).view(np.uint8)
    words = codes.reshape(n // 512, 128, 4, m).transpose(0, 1, 3, 2)
    return np.ascontiguousarray(words), np.ascontiguousarray(byte.astype(np.uint8).reshape(n // 512, 16, m))


N, D, F = 512, 1024, 1024


def logistic(g):
    return 1.0 / (1.0 + np.exp(-g))


def setup_inputs():
    s, t = mx_kscale(D), mx_kscale(F)
    x = bf(np.random.standard_normal((N, D)) * s)
    dx = bf(np.random.standard_normal((N, D)) * s)
    wg_words, wg_scales = pack4(np.random.standard_normal((D, F)) / np.sqrt(D) / s[:, None])
    wu_words, wu_scales = pack4(np.random.standard_normal((D, F)) / np.sqrt(D) / s[:, None] * t)
    wd_words, wd_scales = pack4(np.random.standard_normal((F, D)) / np.sqrt(F) / t[:, None])
    return {"x": x,
            "dx": dx,
            "wg_words": wg_words, "wg_scales": wg_scales,
            "wu_words": wu_words, "wu_scales": wu_scales,
            "wd_words": wd_words, "wd_scales": wd_scales}


def core(x, dx, wg_words, wg_scales, wu_words, wu_scales, wd_words, wd_scales):
    xq = mxq(f64(x), 1, "e4m3")
    dxq = mxq(f64(dx), 1, "e4m3")
    wgq = unpack4(wg_words, wg_scales)
    wuq = unpack4(wu_words, wu_scales)
    g = xq @ wgq
    dg = dxq @ wgq
    u = xq @ wuq
    du = dxq @ wuq
    s = logistic(g)
    sp = s * (1.0 + g * (1.0 - s))
    dh = sp * dg * u + g * s * du
    return mxq(dh, 1, "e4m3") @ unpack4(wd_words, wd_scales)


def reference(x, dx, wg_words, wg_scales, wu_words, wu_scales, wd_words, wd_scales):
    R_out = core(x, dx, wg_words, wg_scales, wu_words, wu_scales, wd_words, wd_scales)
    words, scales = planes(R_out)
    return R_out, words, scales

@@ -1,0 +1,387 @@
+from contextlib import ExitStack
+
+import concourse.mybir as mybir
+from concourse.masks import make_identity
+
+F32 = mybir.dt.float32
+BF16 = mybir.dt.bfloat16
+U32 = mybir.dt.uint32
+I32 = mybir.dt.int32
+U8 = mybir.dt.uint8
+FP8X4 = mybir.dt.float8_e4m3fn_x4
+FP4X4 = mybir.dt.float4_e2m1fn_x4
+ADD = mybir.AluOpType.add
+SUB = mybir.AluOpType.subtract
+MUL = mybir.AluOpType.mult
+ACT = mybir.ActivationFunctionType
+
+FLOPS = 5 * 2 * 512 * 1024 * 1024
+
+P = 128
+T = 4
+K = 1024
+G = 2
+H = 512
+
+
+def tile_swigluforwardtangentjvp_x2_kernel(
+    tc, x, dx, wg_words, wg_scales, wu_words, wu_scales, wd_words, wd_scales, out_0, out_1, out_2
+):
+    nc = tc.nc
+    with ExitStack() as ctx:
+        keep = ctx.enter_context(tc.tile_pool(name="keep", bufs=1))
+        work = ctx.enter_context(tc.tile_pool(name="work", bufs=2))
+        psum = ctx.enter_context(tc.psum_pool(name="psum", bufs=1))
+        ctx.enter_context(tc.manual_schedule())
+
+        x_rows = x.rearrange("(p t) k -> p t k", t=T)
+        dx_rows = dx.rearrange("(p t) k -> p t k", t=T)
+        y_rows = out_0.rearrange("(p t) m -> p t m", t=T)
+
+        planes = {}
+        for n in ("wg", "wu", "wd"):
+            planes[n] = keep.tile([P, G, K], U8, name="plane_" + n, align_bytes=64)
+            nc.vector.memset(planes[n][:].rearrange("p g n -> p (g n)").bitcast(I32), 0)
+        ident = keep.tile([P, P], F32, name="ident")
+        make_identity(nc, ident[:])
+        dummy = keep.tile([P, 1], F32, name="dummy")
+        nc.vector.memset(dummy[:], 0.0)
+        nc.scalar.activation(out=dummy[:], in_=dummy[:], func=ACT.Silu)
+
+        xin = {}
+
+        def load_x(t):
+            for nm, src in (("x", x_rows), ("d", dx_rows)):
+                xin[nm, t] = keep.tile([P, K], BF16, name="in_%s%d" % (nm, t), align_bytes=64)
+                nc.sync.dma_start(out=xin[nm, t][:], in_=src[:, t, :])
+
+        words = {}
+
+        def load_w(n, src, half):
+            words[n, half] = keep.tile([P, G, K], U8, name="w_%s%d" % (n, half), align_bytes=64)
+            nc.sync.dma_start(
+                out=words[n, half][:].bitcast(I32),
+                in_=src.rearrange("g p b -> p g b")[:, :, half * K : (half + 1) * K].bitcast(I32),
+            )
+
+        def load_s(n, src):
+            for q in range(4):
+                nc.sync.dma_start(
+                    out=planes[n][32 * q : 32 * q + 4, :, :].bitcast(I32),
+                    in_=src[:, 4 * q : 4 * q + 4, :].rearrange("g q n -> q g n").bitcast(I32),
+                )
+
+        load_x(0)
+        load_s("wg", wg_scales)
+        load_x(1)
+        load_w("wg", wg_words, 0)
+        load_s("wu", wu_scales)
+        load_w("wu", wu_words, 0)
+        load_w("wg", wg_words, 1)
+        load_w("wu", wu_words, 1)
+        load_x(2)
+        load_x(3)
+        load_s("wd", wd_scales)
+        load_w("wd", wd_words, 0)
+        load_w("wd", wd_words, 1)
+
+        codes = {}
+        scales = {}
+        raw = {}
+
+        def t_pe(t, nm):
+            bank = psum.tile([P, 4, P], F32, name="aux", bufs=2)
+            raw[nm, t] = bank
+            w = xin[nm, t][:].bitcast(F32)
+            for g in range(G):
+                for u in range(2):
+                    nc.tensor.transpose(bank[:, 2 * g + u, :], w[:, 256 * g + u : 256 * (g + 1) : 2], ident[:])
+
+        def t_copy(t, nm, eng):
+            grp = work.tile([P, G * P * 4], BF16, name="xg" + nm, bufs=2, align_bytes=64)
+            o = grp[:].bitcast(F32).rearrange("p (g r u) -> p g r u", g=G, u=2)
+            i = raw[nm, t][:].rearrange("p (g u) r -> p g r u", g=G)
+            if eng == "S":
+                nc.scalar.copy(out=o, in_=i)
+            else:
+                nc.vector.tensor_copy(out=o, in_=i)
+            raw[nm, t] = grp
+
+        def alloc(t, nm):
+            codes[nm, t] = keep.tile([P, G, P], U32, name="c_%s%d" % (nm, t), align_bytes=64)
+            scales[nm, t] = keep.tile([P, G, P], U8, name="s_%s%d" % (nm, t), align_bytes=64)
+
+        def h_pe(t, nm, g, tag, bufs):
+            b = psum.tile([P, 2, P], F32, name=tag, bufs=bufs)
+            raw[nm, t, g] = b
+            for u in range(2):
+                if nm == "h":
+                    w = ew["dh", 2 * t + g][:].rearrange("p u q e -> p (u q e)").bitcast(F32)[:, P * u : P * (u + 1)]
+                else:
+                    w = xin[nm, t][:].bitcast(F32)[:, 256 * g + u : 256 * (g + 1) : 2]
+                nc.tensor.transpose(b[:, u, :], w, ident[:])
+
+        def h_copy(t, nm, g, eng):
+            grp = work.tile([P, P * 4], BF16, name="hg", bufs=4, align_bytes=64)
+            o = grp[:].bitcast(F32).rearrange("p (r u) -> p r u", u=2)
+            i = raw[nm, t, g][:].rearrange("p u r -> p r u")
+            if eng == "S":
+                nc.scalar.copy(out=o, in_=i)
+            else:
+                nc.vector.tensor_copy(out=o, in_=i)
+            raw[nm, t, g] = grp
+
+        def h_quant(t, nm, g):
+            nc.vector.quantize_mx(
+                out=codes[nm, t][:, g, :].bitcast(FP8X4), scales=scales[nm, t][:, g, :], in_=raw[nm, t, g][:]
+            )
+
+        def t_quant(t, nm):
+            alloc(t, nm)
+            nc.vector.quantize_mx(
+                out=codes[nm, t][:].rearrange("p g r -> p (g r)").bitcast(FP8X4),
+                scales=scales[nm, t][:].rearrange("p g r -> p (g r)"),
+                in_=raw[nm, t][:],
+            )
+
+        bank = {}
+        PROD = {"g": ("x", "wg"), "dg": ("d", "wg"), "u": ("x", "wu"), "du": ("d", "wu")}
+
+        def s1(i, which):
+            t, h = divmod(i, 2)
+            nm, wn = PROD[which]
+            b = psum.tile([P, H], F32, name="s1", bufs=6)
+            bank[which, i] = b
+            for g in range(G):
+                nc.tensor.matmul_mx(
+                    out=b[:],
+                    lhsT=codes[nm, t][:, g, :].bitcast(FP8X4),
+                    lhsT_scale=scales[nm, t][:, g, :],
+                    rhs=words[wn, h][:, g, :].bitcast(FP4X4),
+                    rhs_scale=planes[wn][:, g, h * H : (h + 1) * H],
+                    start=(g == 0),
+                    stop=(g == G - 1),
+                )
+
+        ew = {}
+
+        def act(i):
+            ew["th", i] = work.tile([P, H], F32, name="th", bufs=3)
+            nc.scalar.activation(out=ew["th", i][:], in_=bank["g", i][:], func=ACT.Tanh, scale=0.5)
+            ew["sil", i] = work.tile([P, H], F32, name="sil", bufs=3)
+            nc.scalar.activation(out=ew["sil", i][:], in_=bank["g", i][:], func=ACT.Silu)
+
+        def sbar(i):
+            ew["sb", i] = work.tile([P, H], F32, name="sb", bufs=3)
+            nc.gpsimd.tensor_scalar(out=ew["sb", i][:], in0=ew["th", i][:], scalar1=0.5, scalar2=0.5, op0=MUL, op1=SUB)
+
+        def v_d(i):
+            ew["d", i] = work.tile([P, H], F32, name="vd", bufs=2)
+            nc.vector.tensor_tensor(out=ew["d", i][:], in0=ew["sil", i][:], in1=bank["du", i][:], op=MUL)
+
+        def v_c(i):
+            ew["c", i] = work.tile([P, H], F32, name="vc", bufs=2)
+            nc.vector.scalar_tensor_tensor(
+                out=ew["c", i][:], in0=ew["sil", i][:], scalar=1.0, in1=ew["sb", i][:], op0=SUB, op1=MUL
+            )
+
+        def v_a(i):
+            ew["a", i] = work.tile([P, H], F32, name="va", bufs=2)
+            nc.vector.scalar_tensor_tensor(
+                out=ew["a", i][:], in0=ew["c", i][:], scalar=1.0, in1=bank["dg", i][:], op0=SUB, op1=MUL
+            )
+
+        def v_b(i):
+            ew["b", i] = work.tile([P, H], F32, name="vb", bufs=2)
+            nc.vector.tensor_tensor(out=ew["b", i][:], in0=ew["a", i][:], in1=bank["u", i][:], op=MUL)
+
+        def v_add(i):
+            t, h = divmod(i, 2)
+            ew["dh", i] = work.tile([P, 2, P, 2], BF16, name="dh", bufs=4, align_bytes=64)
+            nc.vector.tensor_tensor(
+                out=ew["dh", i][:],
+                in0=ew["d", i][:].rearrange("p (q u e) -> p u q e", u=2, e=2),
+                in1=ew["b", i][:].rearrange("p (q u e) -> p u q e", u=2, e=2),
+                op=SUB,
+            )
+
+        def d_pe(i):
+            t, h = divmod(i, 2)
+            if h == 0:
+                raw["h", t] = psum.tile([P, 4, P], F32, name="aux", bufs=2)
+            w = ew["dh", i][:].rearrange("p u q e -> p (u q e)").bitcast(F32)
+            for u in range(2):
+                nc.tensor.transpose(raw["h", t][:, 2 * h + u, :], w[:, P * u : P * (u + 1)], ident[:])
+
+        def d_copy(t, eng="S"):
+            t_copy(t, "h", eng)
+
+        def d_quant(t):
+            t_quant(t, "h")
+
+        y = keep.tile([P, T, K], F32, name="y", align_bytes=64)
+
+        def s2(t, m):
+            b = psum.tile([P, H], F32, name="aux", bufs=2)
+            bank["y%d" % m, t] = b
+            for g in range(G):
+                nc.tensor.matmul_mx(
+                    out=b[:],
+                    lhsT=codes["h", t][:, g, :].bitcast(FP8X4),
+                    lhsT_scale=scales["h", t][:, g, :],
+                    rhs=words["wd", m][:, g, :].bitcast(FP4X4),
+                    rhs_scale=planes["wd"][:, g, m * H : (m + 1) * H],
+                    start=(g == 0),
+                    stop=(g == G - 1),
+                )
+
+        def y_copy(t, m, eng="S"):
+            o = y[:, t, m * H : (m + 1) * H]
+            if eng == "S":
+                nc.scalar.copy(out=o, in_=bank["y%d" % m, t][:])
+            else:
+                nc.vector.tensor_copy(out=o, in_=bank["y%d" % m, t][:])
+
+        def y_store(t):
+            nc.sync.dma_start(out=y_rows[:, t, :], in_=y[:, t, :])
+
+        def s1_all(i):
+            for w in ("g", "du", "dg", "u"):
+                s1(i, w)
+            act(i)
+            sbar(i)
+
+        def t_all(t, e0="S", e1="S"):
+            t_pe(t, "x")
+            t_pe(t, "d")
+            t_copy(t, "x", e0)
+            t_copy(t, "d", e1)
+
+        def qx(t):
+            t_quant(t, "x")
+
+        def qd(t):
+            t_quant(t, "d")
+
+        def s2_all(t, e0="S", e1="S"):
+            s2(t, 0)
+            s2(t, 1)
+            y_copy(t, 0, e0)
+            y_copy(t, 1, e1)
+            y_store(t)
+
+        def s2_tail(t):
+            for m in range(2):
+                bank["y%d" % m, t] = psum.tile([P, H], F32, name="aux", bufs=2)
+            for g in range(G):
+                for m in range(2):
+                    nc.tensor.matmul_mx(
+                        out=bank["y%d" % m, t][:],
+                        lhsT=codes["h", t][:, g, :].bitcast(FP8X4),
+                        lhsT_scale=scales["h", t][:, g, :],
+                        rhs=words["wd", m][:, g, :].bitcast(FP4X4),
+                        rhs_scale=planes["wd"][:, g, m * H : (m + 1) * H],
+                        start=(g == 0),
+                        stop=(g == G - 1),
+                    )
+            y_copy(t, 0, "S")
+            y_copy(t, 1, "V")
+            y_store(t)
+
+        def d_all(t):
+            d_pe(2 * t)
+            d_pe(2 * t + 1)
+            d_copy(t)
+
+        def vec(i, after_c=(), after_b=()):
+            v_c(i)
+            for f, z in after_c:
+                f(z)
+            v_d(i)
+            v_a(i)
+            if i > 0:
+                v_add(i - 1)
+            v_b(i)
+            for f, z in after_b:
+                f(z)
+
+        alloc(0, "x")
+        alloc(0, "d")
+        for nm in ("x", "d"):
+            for g in range(G):
+                h_pe(0, nm, g, "s1", 6)
+        h_copy(0, "x", 0, "S")
+        h_copy(0, "x", 1, "V")
+        h_copy(0, "d", 0, "S")
+        h_quant(0, "x", 0)
+        h_copy(0, "d", 1, "V")
+        h_quant(0, "x", 1)
+        h_quant(0, "d", 0)
+        h_quant(0, "d", 1)
+        s1_all(0)
+        t_all(1)
+        vec(0, after_b=((qx, 1), (qd, 1)))
+        s1_all(1)
+        vec(1)
+        s1_all(2)
+        t_all(2)
+        vec(2, after_b=((qx, 2), (qd, 2)))
+        s1_all(3)
+        vec(3)
+        s1_all(4)
+        t_all(3)
+        d_all(0)
+        vec(4, after_b=((qx, 3), (qd, 3), (d_quant, 0)))
+        s1_all(5)
+        s2_all(0)
+        vec(5)
+        s1_all(6)
+        d_all(1)
+        vec(6, after_b=((d_quant, 1),))
+        s1(7, "g")
+        s1(7, "du")
+        act(7)
+        sbar(7)
+        d_all(2)
+        s1(7, "dg")
+        s1(7, "u")
+        s2_all(1)
+        vec(7, after_c=((d_quant, 2),))
+        v_add(7)
+        s2_all(2)
+        alloc(3, "h")
+        h_pe(3, "h", 0, "s1", 6)
+        h_pe(3, "h", 1, "s1", 6)
+        h_copy(3, "h", 0, "S")
+        h_quant(3, "h", 0)
+        h_copy(3, "h", 1, "V")
+        h_quant(3, "h", 1)
+        s2_tail(3)
+
+        yb = keep.tile([P, K, T], BF16, name="yb", align_bytes=64)
+        yc = keep.tile([P, K], U32, name="yc", align_bytes=64)
+        ys = keep.tile([P, K], U8, name="ys", align_bytes=64)
+        CH = 512
+        for n, (lo, eng) in enumerate(((0, "V"), (256, "S"), (512, "V"), (768, "S"))):
+            sl = slice(lo, lo + 256)
+            o = yb[:, sl, :]
+            i = y[:, :, sl].rearrange("p t m -> p m t")
+            if eng == "S":
+                nc.scalar.copy(out=o, in_=i)
+            else:
+                nc.vector.tensor_copy(out=o, in_=i)
+        for c in range(0, K, CH):
+            nc.vector.quantize_mx(
+                out=yc[:, c : c + CH].bitcast(FP8X4),
+                scales=ys[:, c : c + CH],
+                in_=yb[:, c : c + CH, :].rearrange("p m t -> p (m t)"),
+            )
+            nc.sync.dma_start(
+                out=out_1[0].rearrange("p m t -> p (m t)")[:, 4 * c : 4 * (c + CH)].bitcast(I32),
+                in_=yc[:, c : c + CH].bitcast(I32),
+            )
+        for q in range(4):
+            nc.sync.dma_start(
+                out=out_2[0, 4 * q : 4 * q + 4, :].bitcast(I32),
+                in_=ys[32 * q : 32 * q + 4, :].bitcast(I32),
+            )

@@ -73,12 +73,12 @@ def tile_swigluforwardtangentjvp_x2_kernel(
 
         load_x(0)
         load_s("wg", wg_scales)
-        load_x(1)
         load_w("wg", wg_words, 0)
-        load_s("wu", wu_scales)
         load_w("wu", wu_words, 0)
+        load_s("wu", wu_scales)
         load_w("wg", wg_words, 1)
         load_w("wu", wu_words, 1)
+        load_x(1)
         load_x(2)
         load_x(3)
         load_s("wd", wd_scales)
@@ -165,44 +165,42 @@ def tile_swigluforwardtangentjvp_x2_kernel(
 
         ew = {}
 
+        def perm(ap):
+            return ap.rearrange("p (q u e) -> p u q e", u=2, e=2)
+
         def act(i):
-            ew["th", i] = work.tile([P, H], F32, name="th", bufs=3)
-            nc.scalar.activation(out=ew["th", i][:], in_=bank["g", i][:], func=ACT.Tanh, scale=0.5)
-            ew["sil", i] = work.tile([P, H], F32, name="sil", bufs=3)
-            nc.scalar.activation(out=ew["sil", i][:], in_=bank["g", i][:], func=ACT.Silu)
-
-        def sbar(i):
-            ew["sb", i] = work.tile([P, H], F32, name="sb", bufs=3)
-            nc.gpsimd.tensor_scalar(out=ew["sb", i][:], in0=ew["th", i][:], scalar1=0.5, scalar2=0.5, op0=MUL, op1=SUB)
-
-        def v_d(i):
-            ew["d", i] = work.tile([P, H], F32, name="vd", bufs=2)
-            nc.vector.tensor_tensor(out=ew["d", i][:], in0=ew["sil", i][:], in1=bank["du", i][:], op=MUL)
-
-        def v_c(i):
-            ew["c", i] = work.tile([P, H], F32, name="vc", bufs=2)
-            nc.vector.scalar_tensor_tensor(
-                out=ew["c", i][:], in0=ew["sil", i][:], scalar=1.0, in1=ew["sb", i][:], op0=SUB, op1=MUL
-            )
+            g = bank["g", i]
+            ew["r", i] = work.tile([P, H], F32, name="r", bufs=3)
+            nc.scalar.activation(out=ew["r", i][:], in_=g[:], func=ACT.Silu, scale=-1.0)
+            ew["h", i] = work.tile([P, H], F32, name="h", bufs=3)
+            nc.scalar.activation(out=ew["h", i][:], in_=g[:], func=ACT.Copy, scale=0.5)
+            ew["th", i] = work.tile([P, 2, P, 2], F32, name="th", bufs=4)
+            nc.scalar.activation(out=ew["th", i][:], in_=perm(g[:]), func=ACT.Tanh, scale=0.5)
 
         def v_a(i):
             ew["a", i] = work.tile([P, H], F32, name="va", bufs=2)
             nc.vector.scalar_tensor_tensor(
-                out=ew["a", i][:], in0=ew["c", i][:], scalar=1.0, in1=bank["dg", i][:], op0=SUB, op1=MUL
+                out=ew["a", i][:], in0=ew["r", i][:], scalar=1.0, in1=bank["dg", i][:], op0=SUB, op1=MUL
             )
 
-        def v_b(i):
-            ew["b", i] = work.tile([P, H], F32, name="vb", bufs=2)
-            nc.vector.tensor_tensor(out=ew["b", i][:], in0=ew["a", i][:], in1=bank["u", i][:], op=MUL)
+        def v_f(i):
+            ew["f", i] = work.tile([P, 2, P, 2], F32, name="vf", bufs=2)
+            nc.vector.tensor_tensor(out=ew["f", i][:], in0=perm(ew["h", i][:]), in1=perm(bank["du", i][:]), op=MUL)
 
-        def v_add(i):
-            t, h = divmod(i, 2)
+        def v_b(i):
+            ew["b", i] = work.tile([P, 2, P, 2], F32, name="vb", bufs=2)
+            nc.vector.tensor_tensor(out=ew["b", i][:], in0=perm(ew["a", i][:]), in1=perm(bank["u", i][:]), op=MUL)
+
+        def v_l(i):
+            ew["l", i] = work.tile([P, 2, P, 2], F32, name="vl", bufs=2)
+            nc.vector.scalar_tensor_tensor(
+                out=ew["l", i][:], in0=ew["b", i][:], scalar=-0.5, in1=ew["f", i][:], op0=MUL, op1=ADD
+            )
+
+        def v_dh(i):
             ew["dh", i] = work.tile([P, 2, P, 2], BF16, name="dh", bufs=4, align_bytes=64)
-            nc.vector.tensor_tensor(
-                out=ew["dh", i][:],
-                in0=ew["d", i][:].rearrange("p (q u e) -> p u q e", u=2, e=2),
-                in1=ew["b", i][:].rearrange("p (q u e) -> p u q e", u=2, e=2),
-                op=SUB,
+            nc.vector.scalar_tensor_tensor(
+                out=ew["dh", i][:], in0=ew["th", i][:], scalar=1.0, in1=ew["l", i][:], op0=ADD, op1=MUL
             )
 
         def d_pe(i):
@@ -246,10 +244,9 @@ def tile_swigluforwardtangentjvp_x2_kernel(
             nc.sync.dma_start(out=y_rows[:, t, :], in_=y[:, t, :])
 
         def s1_all(i):
-            for w in ("g", "du", "dg", "u"):
+            for w in ("g", "dg", "du", "u"):
                 s1(i, w)
             act(i)
-            sbar(i)
 
         def t_all(t, e0="S", e1="S"):
             t_pe(t, "x")
@@ -272,7 +269,7 @@ def tile_swigluforwardtangentjvp_x2_kernel(
 
         def s2_tail(t):
             for m in range(2):
-                bank["y%d" % m, t] = psum.tile([P, H], F32, name="aux", bufs=2)
+                bank["y%d" % m, t] = psum.tile([P, H], F32, name="s1", bufs=6)
             for g in range(G):
                 for m in range(2):
                     nc.tensor.matmul_mx(
@@ -288,22 +285,32 @@ def tile_swigluforwardtangentjvp_x2_kernel(
             y_copy(t, 1, "V")
             y_store(t)
 
+        yb = keep.tile([P, K, T], BF16, name="yb", align_bytes=64)
+
+        def inter(t, lo, hi, eng):
+            o = yb[:, lo:hi, t : t + 2]
+            i = y[:, t : t + 2, lo:hi].rearrange("p t m -> p m t")
+            if eng == "S":
+                nc.scalar.copy(out=o, in_=i)
+            else:
+                nc.vector.tensor_copy(out=o, in_=i)
+
         def d_all(t):
             d_pe(2 * t)
             d_pe(2 * t + 1)
             d_copy(t)
 
-        def vec(i, after_c=(), after_b=()):
-            v_c(i)
-            for f, z in after_c:
-                f(z)
-            v_d(i)
+        def vec(i, after_a=(), after_b=()):
             v_a(i)
-            if i > 0:
-                v_add(i - 1)
+            for f, z in after_a:
+                f(z)
+            v_f(i)
             v_b(i)
+            if i > 0:
+                v_dh(i - 1)
             for f, z in after_b:
                 f(z)
+            v_l(i)
 
         alloc(0, "x")
         alloc(0, "d")
@@ -319,10 +326,10 @@ def tile_swigluforwardtangentjvp_x2_kernel(
         h_quant(0, "d", 0)
         h_quant(0, "d", 1)
         s1_all(0)
-        t_all(1)
-        vec(0, after_b=((qx, 1), (qd, 1)))
+        vec(0)
         s1_all(1)
-        vec(1)
+        t_all(1)
+        vec(1, after_b=((qx, 1), (qd, 1)))
         s1_all(2)
         t_all(2)
         vec(2, after_b=((qx, 2), (qd, 2)))
@@ -339,37 +346,36 @@ def tile_swigluforwardtangentjvp_x2_kernel(
         d_all(1)
         vec(6, after_b=((d_quant, 1),))
         s1(7, "g")
-        s1(7, "du")
-        act(7)
-        sbar(7)
-        d_all(2)
         s1(7, "dg")
+        act(7)
+        d_all(2)
+        s1(7, "du")
         s1(7, "u")
         s2_all(1)
-        vec(7, after_c=((d_quant, 2),))
-        v_add(7)
-        s2_all(2)
+        vec(7, after_b=((d_quant, 2),))
+        v_dh(7)
+        inter(0, 0, H, "V")
+        s2(2, 0)
+        s2(2, 1)
+        y_copy(2, 0)
         alloc(3, "h")
         h_pe(3, "h", 0, "s1", 6)
         h_pe(3, "h", 1, "s1", 6)
         h_copy(3, "h", 0, "S")
         h_quant(3, "h", 0)
-        h_copy(3, "h", 1, "V")
+        h_copy(3, "h", 1, "S")
         h_quant(3, "h", 1)
+        y_copy(2, 1)
+        y_store(2)
+        inter(0, H, K, "V")
         s2_tail(3)
 
-        yb = keep.tile([P, K, T], BF16, name="yb", align_bytes=64)
         yc = keep.tile([P, K], U32, name="yc", align_bytes=64)
         ys = keep.tile([P, K], U8, name="ys", align_bytes=64)
         CH = 512
-        for n, (lo, eng) in enumerate(((0, "V"), (256, "S"), (512, "V"), (768, "S"))):
-            sl = slice(lo, lo + 256)
-            o = yb[:, sl, :]
-            i = y[:, :, sl].rearrange("p t m -> p m t")
-            if eng == "S":
-                nc.scalar.copy(out=o, in_=i)
-            else:
-                nc.vector.tensor_copy(out=o, in_=i)
+        inter(2, 640, K, "S")
+        inter(2, 0, 384, "V")
+        inter(2, 384, 640, "V")
         for c in range(0, K, CH):
             nc.vector.quantize_mx(
                 out=yc[:, c : c + CH].bitcast(FP8X4),

@@ -34,8 +34,6 @@ def tile_swigluforwardtangentjvp_x2_kernel(
         psum = ctx.enter_context(tc.psum_pool(name="psum", bufs=1))
         ctx.enter_context(tc.manual_schedule())
 
-        x_rows = x.rearrange("(p t) k -> p t k", t=T)
-        dx_rows = dx.rearrange("(p t) k -> p t k", t=T)
         y_rows = out_0.rearrange("(p t) m -> p t m", t=T)
 
         planes = {}
@@ -44,16 +42,15 @@ def tile_swigluforwardtangentjvp_x2_kernel(
             nc.vector.memset(planes[n][:].rearrange("p g n -> p (g n)").bitcast(I32), 0)
         ident = keep.tile([P, P], F32, name="ident")
         make_identity(nc, ident[:])
-        dummy = keep.tile([P, 1], F32, name="dummy")
-        nc.vector.memset(dummy[:], 0.0)
-        nc.scalar.activation(out=dummy[:], in_=dummy[:], func=ACT.Silu)
 
         xin = {}
 
-        def load_x(t):
-            for nm, src in (("x", x_rows), ("d", dx_rows)):
-                xin[nm, t] = keep.tile([P, K], BF16, name="in_%s%d" % (nm, t), align_bytes=64)
-                nc.sync.dma_start(out=xin[nm, t][:], in_=src[:, t, :])
+        def load_x(t, n):
+            for nm, src in (("x", x), ("d", dx)):
+                b = keep.tile([P, n, K], BF16, name="in_%s%d" % (nm, t), align_bytes=64)
+                nc.sync.dma_start(out=b[:], in_=src.rearrange("(p t) k -> p t k", t=T)[:, t : t + n, :])
+                for s in range(n):
+                    xin[nm, t + s] = b[:, s, :]
 
         words = {}
 
@@ -64,99 +61,94 @@ def tile_swigluforwardtangentjvp_x2_kernel(
                 in_=src.rearrange("g p b -> p g b")[:, :, half * K : (half + 1) * K].bitcast(I32),
             )
 
-        def load_s(n, src):
+        def load_s(n, src, eng):
             for q in range(4):
-                nc.sync.dma_start(
+                eng.dma_start(
                     out=planes[n][32 * q : 32 * q + 4, :, :].bitcast(I32),
                     in_=src[:, 4 * q : 4 * q + 4, :].rearrange("g q n -> q g n").bitcast(I32),
                 )
 
-        load_x(0)
-        load_s("wg", wg_scales)
+        load_s("wg", wg_scales, nc.scalar)
+        load_x(0, 1)
         load_w("wg", wg_words, 0)
         load_w("wu", wu_words, 0)
-        load_s("wu", wu_scales)
+        load_s("wu", wu_scales, nc.sync)
         load_w("wg", wg_words, 1)
         load_w("wu", wu_words, 1)
-        load_x(1)
-        load_x(2)
-        load_x(3)
-        load_s("wd", wd_scales)
+        load_x(1, 1)
+        load_x(2, 2)
+        load_s("wd", wd_scales, nc.sync)
         load_w("wd", wd_words, 0)
         load_w("wd", wd_words, 1)
+        warm = keep.tile([P, 1], F32, name="warm")
+        nc.vector.memset(warm[:], 0.0)
+        nc.scalar.activation(out=warm[:], in_=warm[:], func=ACT.Silu)
 
         codes = {}
         scales = {}
         raw = {}
 
-        def t_pe(t, nm):
-            bank = psum.tile([P, 4, P], F32, name="aux", bufs=2)
-            raw[nm, t] = bank
-            w = xin[nm, t][:].bitcast(F32)
-            for g in range(G):
-                for u in range(2):
-                    nc.tensor.transpose(bank[:, 2 * g + u, :], w[:, 256 * g + u : 256 * (g + 1) : 2], ident[:])
-
-        def t_copy(t, nm, eng):
-            grp = work.tile([P, G * P * 4], BF16, name="xg" + nm, bufs=2, align_bytes=64)
-            o = grp[:].bitcast(F32).rearrange("p (g r u) -> p g r u", g=G, u=2)
-            i = raw[nm, t][:].rearrange("p (g u) r -> p g r u", g=G)
+        def copy(eng, out, in_):
             if eng == "S":
-                nc.scalar.copy(out=o, in_=i)
+                nc.scalar.copy(out=out, in_=in_)
             else:
-                nc.vector.tensor_copy(out=o, in_=i)
-            raw[nm, t] = grp
+                nc.vector.tensor_copy(out=out, in_=in_)
 
-        def alloc(t, nm):
-            codes[nm, t] = keep.tile([P, G, P], U32, name="c_%s%d" % (nm, t), align_bytes=64)
-            scales[nm, t] = keep.tile([P, G, P], U8, name="s_%s%d" % (nm, t), align_bytes=64)
+        def x_alloc(t):
+            raw["x", t] = work.tile([P, 2, G, P * 4], BF16, name="xgrp", bufs=2, align_bytes=64)
+            codes["x", t] = keep.tile([P, 2, G, P], U32, name="cx%d" % t, align_bytes=64)
+            scales["x", t] = keep.tile([P, 2, G, P], U8, name="sx%d" % t, align_bytes=64)
 
-        def h_pe(t, nm, g, tag, bufs):
-            b = psum.tile([P, 2, P], F32, name=tag, bufs=bufs)
-            raw[nm, t, g] = b
+        def x_pe(t, j, g, b, s):
+            w = xin["xd"[j], t].bitcast(F32)
             for u in range(2):
-                if nm == "h":
-                    w = ew["dh", 2 * t + g][:].rearrange("p u q e -> p (u q e)").bitcast(F32)[:, P * u : P * (u + 1)]
-                else:
-                    w = xin[nm, t][:].bitcast(F32)[:, 256 * g + u : 256 * (g + 1) : 2]
-                nc.tensor.transpose(b[:, u, :], w, ident[:])
+                nc.tensor.transpose(b[:, s + u, :], w[:, 256 * g + u : 256 * (g + 1) : 2], ident[:])
 
-        def h_copy(t, nm, g, eng):
-            grp = work.tile([P, P * 4], BF16, name="hg", bufs=4, align_bytes=64)
-            o = grp[:].bitcast(F32).rearrange("p (r u) -> p r u", u=2)
-            i = raw[nm, t, g][:].rearrange("p u r -> p r u")
-            if eng == "S":
-                nc.scalar.copy(out=o, in_=i)
-            else:
-                nc.vector.tensor_copy(out=o, in_=i)
-            raw[nm, t, g] = grp
+        half = {}
 
-        def h_quant(t, nm, g):
-            nc.vector.quantize_mx(
-                out=codes[nm, t][:, g, :].bitcast(FP8X4), scales=scales[nm, t][:, g, :], in_=raw[nm, t, g][:]
+        def x_half_pe(t, j, g):
+            half[t, j, g] = psum.tile([P, 2, P], F32, name="s1", bufs=6)
+            x_pe(t, j, g, half[t, j, g], 0)
+
+        def x_half_copy(t, j, g, eng):
+            copy(
+                eng,
+                raw["x", t][:, j, g, :].bitcast(F32).rearrange("p (r u) -> p r u", u=2),
+                half[t, j, g][:].rearrange("p u r -> p r u"),
             )
 
-        def t_quant(t, nm):
-            alloc(t, nm)
-            nc.vector.quantize_mx(
-                out=codes[nm, t][:].rearrange("p g r -> p (g r)").bitcast(FP8X4),
-                scales=scales[nm, t][:].rearrange("p g r -> p (g r)"),
-                in_=raw[nm, t][:],
+        def x_full(t, j, eng, tag, bufs):
+            b = psum.tile([P, 4, P], F32, name=tag, bufs=bufs)
+            for g in range(G):
+                x_pe(t, j, g, b, 2 * g)
+            copy(
+                eng,
+                raw["x", t][:, j, :, :].rearrange("p g n -> p (g n)").bitcast(F32).rearrange("p (g r u) -> p g r u", g=G, u=2),
+                b[:].rearrange("p (g u) r -> p g r u", g=G),
             )
+
+        def x_quant(t, sel):
+            nc.vector.quantize_mx(
+                out=codes["x", t][:, sel].rearrange("p j g r -> p (j g r)").bitcast(FP8X4),
+                scales=scales["x", t][:, sel].rearrange("p j g r -> p (j g r)"),
+                in_=raw["x", t][:, sel].rearrange("p j g n -> p (j g n)"),
+            )
+
+        BOTH = slice(0, 2)
 
         bank = {}
-        PROD = {"g": ("x", "wg"), "dg": ("d", "wg"), "u": ("x", "wu"), "du": ("d", "wu")}
+        PROD = {"g": (0, "wg"), "dg": (1, "wg"), "u": (0, "wu"), "du": (1, "wu")}
 
         def s1(i, which):
             t, h = divmod(i, 2)
-            nm, wn = PROD[which]
+            j, wn = PROD[which]
             b = psum.tile([P, H], F32, name="s1", bufs=6)
             bank[which, i] = b
             for g in range(G):
                 nc.tensor.matmul_mx(
                     out=b[:],
-                    lhsT=codes[nm, t][:, g, :].bitcast(FP8X4),
-                    lhsT_scale=scales[nm, t][:, g, :],
+                    lhsT=codes["x", t][:, j, g, :].bitcast(FP8X4),
+                    lhsT_scale=scales["x", t][:, j, g, :],
                     rhs=words[wn, h][:, g, :].bitcast(FP4X4),
                     rhs_scale=planes[wn][:, g, h * H : (h + 1) * H],
                     start=(g == 0),
@@ -168,226 +160,220 @@ def tile_swigluforwardtangentjvp_x2_kernel(
         def perm(ap):
             return ap.rearrange("p (q u e) -> p u q e", u=2, e=2)
 
+        def tile(name, i, dt=F32, shape=(P, H), bufs=2):
+            ew[name, i] = work.tile(list(shape), dt, name=name, bufs=bufs, align_bytes=64)
+            return ew[name, i]
+
         def act(i):
             g = bank["g", i]
-            ew["r", i] = work.tile([P, H], F32, name="r", bufs=3)
-            nc.scalar.activation(out=ew["r", i][:], in_=g[:], func=ACT.Silu, scale=-1.0)
-            ew["h", i] = work.tile([P, H], F32, name="h", bufs=3)
-            nc.scalar.activation(out=ew["h", i][:], in_=g[:], func=ACT.Copy, scale=0.5)
-            ew["th", i] = work.tile([P, 2, P, 2], F32, name="th", bufs=4)
-            nc.scalar.activation(out=ew["th", i][:], in_=perm(g[:]), func=ACT.Tanh, scale=0.5)
+            nc.scalar.activation(out=tile("sil", i, bufs=3)[:], in_=g[:], func=ACT.Silu)
+            nc.scalar.activation(out=tile("th", i, bufs=3)[:], in_=g[:], func=ACT.Tanh, scale=0.5)
+            nc.scalar.activation(out=tile("sm", i, bufs=3)[:], in_=ew["sil", i][:], func=ACT.Copy, scale=0.5, bias=-0.5)
+
+        def v_c(i):
+            nc.vector.scalar_tensor_tensor(
+                out=tile("c", i)[:], in0=ew["th", i][:], scalar=1.0, in1=ew["sm", i][:], op0=SUB, op1=MUL
+            )
 
         def v_a(i):
-            ew["a", i] = work.tile([P, H], F32, name="va", bufs=2)
             nc.vector.scalar_tensor_tensor(
-                out=ew["a", i][:], in0=ew["r", i][:], scalar=1.0, in1=bank["dg", i][:], op0=SUB, op1=MUL
+                out=tile("a", i)[:], in0=ew["c", i][:], scalar=1.0, in1=bank["dg", i][:], op0=SUB, op1=MUL
             )
 
-        def v_f(i):
-            ew["f", i] = work.tile([P, 2, P, 2], F32, name="vf", bufs=2)
-            nc.vector.tensor_tensor(out=ew["f", i][:], in0=perm(ew["h", i][:]), in1=perm(bank["du", i][:]), op=MUL)
+        W = (P, 2, P, 2)
+
+        def v_d(i):
+            nc.vector.tensor_tensor(
+                out=tile("d", i, shape=W)[:], in0=perm(ew["sil", i][:]), in1=perm(bank["du", i][:]), op=MUL
+            )
 
         def v_b(i):
-            ew["b", i] = work.tile([P, 2, P, 2], F32, name="vb", bufs=2)
-            nc.vector.tensor_tensor(out=ew["b", i][:], in0=perm(ew["a", i][:]), in1=perm(bank["u", i][:]), op=MUL)
-
-        def v_l(i):
-            ew["l", i] = work.tile([P, 2, P, 2], F32, name="vl", bufs=2)
-            nc.vector.scalar_tensor_tensor(
-                out=ew["l", i][:], in0=ew["b", i][:], scalar=-0.5, in1=ew["f", i][:], op0=MUL, op1=ADD
+            nc.vector.tensor_tensor(
+                out=tile("b", i, shape=W)[:], in0=perm(ew["a", i][:]), in1=perm(bank["u", i][:]), op=MUL
             )
 
-        def v_dh(i):
-            ew["dh", i] = work.tile([P, 2, P, 2], BF16, name="dh", bufs=4, align_bytes=64)
-            nc.vector.scalar_tensor_tensor(
-                out=ew["dh", i][:], in0=ew["th", i][:], scalar=1.0, in1=ew["l", i][:], op0=ADD, op1=MUL
-            )
+        def dh(i, eng):
+            eng.tensor_tensor(out=tile("dh", i, BF16, W, 4)[:], in0=ew["d", i][:], in1=ew["b", i][:], op=SUB)
 
-        def d_pe(i):
-            t, h = divmod(i, 2)
-            if h == 0:
-                raw["h", t] = psum.tile([P, 4, P], F32, name="aux", bufs=2)
-            w = ew["dh", i][:].rearrange("p u q e -> p (u q e)").bitcast(F32)
+        def d_alloc(t):
+            raw["h", t] = work.tile([P, G, P * 4], BF16, name="hgrp", bufs=2, align_bytes=64)
+            codes["h", t] = keep.tile([P, G, P], U32, name="ch%d" % t, align_bytes=64)
+            scales["h", t] = keep.tile([P, G, P], U8, name="sh%d" % t, align_bytes=64)
+
+        def d_pe(t, h, b, s):
+            w = ew["dh", 2 * t + h][:].rearrange("p u q e -> p (u q e)").bitcast(F32)
             for u in range(2):
-                nc.tensor.transpose(raw["h", t][:, 2 * h + u, :], w[:, P * u : P * (u + 1)], ident[:])
+                nc.tensor.transpose(b[:, s + u, :], w[:, P * u : P * (u + 1)], ident[:])
 
-        def d_copy(t, eng="S"):
-            t_copy(t, "h", eng)
+        def d_full(t, eng):
+            d_alloc(t)
+            b = psum.tile([P, 4, P], F32, name="aux", bufs=2)
+            for h in range(2):
+                d_pe(t, h, b, 2 * h)
+            copy(
+                eng,
+                raw["h", t][:].rearrange("p g n -> p (g n)").bitcast(F32).rearrange("p (g r u) -> p g r u", g=G, u=2),
+                b[:].rearrange("p (g u) r -> p g r u", g=G),
+            )
 
-        def d_quant(t):
-            t_quant(t, "h")
+        def d_half(t, h, eng):
+            b = psum.tile([P, 2, P], F32, name="s1", bufs=6)
+            d_pe(t, h, b, 0)
+            copy(
+                eng,
+                raw["h", t][:, h, :].bitcast(F32).rearrange("p (r u) -> p r u", u=2),
+                b[:].rearrange("p u r -> p r u"),
+            )
+
+        def d_quant(t, sel):
+            nc.vector.quantize_mx(
+                out=codes["h", t][:, sel].rearrange("p g r -> p (g r)").bitcast(FP8X4),
+                scales=scales["h", t][:, sel].rearrange("p g r -> p (g r)"),
+                in_=raw["h", t][:, sel].rearrange("p g n -> p (g n)"),
+            )
 
         y = keep.tile([P, T, K], F32, name="y", align_bytes=64)
-
-        def s2(t, m):
-            b = psum.tile([P, H], F32, name="aux", bufs=2)
-            bank["y%d" % m, t] = b
-            for g in range(G):
-                nc.tensor.matmul_mx(
-                    out=b[:],
-                    lhsT=codes["h", t][:, g, :].bitcast(FP8X4),
-                    lhsT_scale=scales["h", t][:, g, :],
-                    rhs=words["wd", m][:, g, :].bitcast(FP4X4),
-                    rhs_scale=planes["wd"][:, g, m * H : (m + 1) * H],
-                    start=(g == 0),
-                    stop=(g == G - 1),
-                )
-
-        def y_copy(t, m, eng="S"):
-            o = y[:, t, m * H : (m + 1) * H]
-            if eng == "S":
-                nc.scalar.copy(out=o, in_=bank["y%d" % m, t][:])
-            else:
-                nc.vector.tensor_copy(out=o, in_=bank["y%d" % m, t][:])
-
-        def y_store(t):
-            nc.sync.dma_start(out=y_rows[:, t, :], in_=y[:, t, :])
-
-        def s1_all(i):
-            for w in ("g", "dg", "du", "u"):
-                s1(i, w)
-            act(i)
-
-        def t_all(t, e0="S", e1="S"):
-            t_pe(t, "x")
-            t_pe(t, "d")
-            t_copy(t, "x", e0)
-            t_copy(t, "d", e1)
-
-        def qx(t):
-            t_quant(t, "x")
-
-        def qd(t):
-            t_quant(t, "d")
-
-        def s2_all(t, e0="S", e1="S"):
-            s2(t, 0)
-            s2(t, 1)
-            y_copy(t, 0, e0)
-            y_copy(t, 1, e1)
-            y_store(t)
-
-        def s2_tail(t):
-            for m in range(2):
-                bank["y%d" % m, t] = psum.tile([P, H], F32, name="s1", bufs=6)
-            for g in range(G):
-                for m in range(2):
-                    nc.tensor.matmul_mx(
-                        out=bank["y%d" % m, t][:],
-                        lhsT=codes["h", t][:, g, :].bitcast(FP8X4),
-                        lhsT_scale=scales["h", t][:, g, :],
-                        rhs=words["wd", m][:, g, :].bitcast(FP4X4),
-                        rhs_scale=planes["wd"][:, g, m * H : (m + 1) * H],
-                        start=(g == 0),
-                        stop=(g == G - 1),
-                    )
-            y_copy(t, 0, "S")
-            y_copy(t, 1, "V")
-            y_store(t)
-
         yb = keep.tile([P, K, T], BF16, name="yb", align_bytes=64)
-
-        def inter(t, lo, hi, eng):
-            o = yb[:, lo:hi, t : t + 2]
-            i = y[:, t : t + 2, lo:hi].rearrange("p t m -> p m t")
-            if eng == "S":
-                nc.scalar.copy(out=o, in_=i)
-            else:
-                nc.vector.tensor_copy(out=o, in_=i)
-
-        def d_all(t):
-            d_pe(2 * t)
-            d_pe(2 * t + 1)
-            d_copy(t)
-
-        def vec(i, after_a=(), after_b=()):
-            v_a(i)
-            for f, z in after_a:
-                f(z)
-            v_f(i)
-            v_b(i)
-            if i > 0:
-                v_dh(i - 1)
-            for f, z in after_b:
-                f(z)
-            v_l(i)
-
-        alloc(0, "x")
-        alloc(0, "d")
-        for nm in ("x", "d"):
-            for g in range(G):
-                h_pe(0, nm, g, "s1", 6)
-        h_copy(0, "x", 0, "S")
-        h_copy(0, "x", 1, "V")
-        h_copy(0, "d", 0, "S")
-        h_quant(0, "x", 0)
-        h_copy(0, "d", 1, "V")
-        h_quant(0, "x", 1)
-        h_quant(0, "d", 0)
-        h_quant(0, "d", 1)
-        s1_all(0)
-        vec(0)
-        s1_all(1)
-        t_all(1)
-        vec(1, after_b=((qx, 1), (qd, 1)))
-        s1_all(2)
-        t_all(2)
-        vec(2, after_b=((qx, 2), (qd, 2)))
-        s1_all(3)
-        vec(3)
-        s1_all(4)
-        t_all(3)
-        d_all(0)
-        vec(4, after_b=((qx, 3), (qd, 3), (d_quant, 0)))
-        s1_all(5)
-        s2_all(0)
-        vec(5)
-        s1_all(6)
-        d_all(1)
-        vec(6, after_b=((d_quant, 1),))
-        s1(7, "g")
-        s1(7, "dg")
-        act(7)
-        d_all(2)
-        s1(7, "du")
-        s1(7, "u")
-        s2_all(1)
-        vec(7, after_b=((d_quant, 2),))
-        v_dh(7)
-        inter(0, 0, H, "V")
-        s2(2, 0)
-        s2(2, 1)
-        y_copy(2, 0)
-        alloc(3, "h")
-        h_pe(3, "h", 0, "s1", 6)
-        h_pe(3, "h", 1, "s1", 6)
-        h_copy(3, "h", 0, "S")
-        h_quant(3, "h", 0)
-        h_copy(3, "h", 1, "S")
-        h_quant(3, "h", 1)
-        y_copy(2, 1)
-        y_store(2)
-        inter(0, H, K, "V")
-        s2_tail(3)
-
         yc = keep.tile([P, K], U32, name="yc", align_bytes=64)
         ys = keep.tile([P, K], U8, name="ys", align_bytes=64)
-        CH = 512
+
+        def s2_mm(t, m, g):
+            nc.tensor.matmul_mx(
+                out=bank["y", t, m][:],
+                lhsT=codes["h", t][:, g, :].bitcast(FP8X4),
+                lhsT_scale=scales["h", t][:, g, :],
+                rhs=words["wd", m][:, g, :].bitcast(FP4X4),
+                rhs_scale=planes["wd"][:, g, m * H : (m + 1) * H],
+                start=(g == 0),
+                stop=(g == G - 1),
+            )
+
+        def s2(t, m):
+            bank["y", t, m] = psum.tile([P, H], F32, name="aux", bufs=2)
+            for g in range(G):
+                s2_mm(t, m, g)
+
+        def y_copy(t, m, eng):
+            copy(eng, y[:, t, m * H : (m + 1) * H], bank["y", t, m][:])
+
+        def y_store(t, lo=0, hi=K):
+            nc.sync.dma_start(out=y_rows[:, t, lo:hi], in_=y[:, t, lo:hi])
+
+        def inter(t, lo, hi, eng):
+            copy(eng, yb[:, lo:hi, t : t + 2], y[:, t : t + 2, lo:hi].rearrange("p t m -> p m t"))
+
+
+        def one(h):
+            return slice(h, h + 1)
+
+        def x_all(t):
+            x_alloc(t)
+            x_full(t, 0, "S", "aux", 2)
+            x_full(t, 1, "S", "aux", 2)
+
+        def s2_all(t):
+            for m in range(2):
+                s2(t, m)
+                y_copy(t, m, "S")
+            y_store(t)
+
+        def step(i, before_dg=(), after_u=(), after_c=(), after_b=()):
+            if i > 0:
+                s1(i, "du")
+                if i + 1 < 8:
+                    s1(i + 1, "g")
+                    act(i + 1)
+                for f in before_dg:
+                    f()
+                s1(i, "dg")
+                s1(i, "u")
+            for f in after_u:
+                f()
+            v_c(i)
+            for f in after_c:
+                f()
+            if i > 0:
+                v_b(i - 1)
+                dh(i - 1, nc.gpsimd)
+            for f in after_b:
+                f()
+            v_d(i)
+            v_a(i)
+
+        x_alloc(0)
+        for j in range(2):
+            for g in range(G):
+                x_half_pe(0, j, g)
+        x_half_copy(0, 0, 0, "S")
+        x_half_copy(0, 0, 1, "V")
+        x_half_copy(0, 1, 0, "S")
+        x_quant(0, one(0))
+        x_half_copy(0, 1, 1, "V")
+        x_quant(0, one(1))
+        s1(0, "g")
+        act(0)
+        s1(0, "dg")
+        s1(0, "du")
+        s1(0, "u")
+        x_all(1)
+        v_d(0)
+        v_c(0)
+        x_quant(1, one(0))
+        v_a(0)
+        x_quant(1, one(1))
+        s1(1, "g")
+        act(1)
+        x_all(2)
+        step(1, after_c=(lambda: x_quant(2, one(0)),), after_b=())
+        x_quant(2, one(1))
+        step(2, after_u=(lambda: x_all(3),))
+        step(3, before_dg=(lambda: d_full(0, "S"),), after_c=(lambda: x_quant(3, BOTH),))
+        step(4)
+        step(5, before_dg=(lambda: d_full(1, "S"),), after_c=(lambda: d_quant(0, BOTH),))
+        s2_all(0)
+        step(6, after_c=(lambda: d_quant(1, BOTH),))
+        step(7)
+        d_full(2, "S")
+        v_b(7)
+        s2_all(1)
+        d_alloc(3)
+        d_half(3, 0, "S")
+        d_quant(2, BOTH)
+        dh(7, nc.vector)
+        s2(2, 0)
+        inter(0, 0, H, "V")
+        d_quant(3, one(0))
+        d_half(3, 1, "S")
+        y_copy(2, 0, "S")
+        s2(2, 1)
+        d_quant(3, one(1))
+        inter(0, H, K, "V")
+        y_copy(2, 1, "S")
+        y_store(2)
+        for m in range(2):
+            bank["y", 3, m] = psum.tile([P, H], F32, name="s1", bufs=6)
+        for g in range(G):
+            for m in range(2):
+                s2_mm(3, m, g)
+        y_copy(3, 0, "S")
+        y_copy(3, 1, "V")
+        y_store(3, 0, H)
+        y_store(3, H, K)
         inter(2, 640, K, "S")
         inter(2, 0, 384, "V")
         inter(2, 384, 640, "V")
-        for c in range(0, K, CH):
+        for c in range(0, K, H):
             nc.vector.quantize_mx(
-                out=yc[:, c : c + CH].bitcast(FP8X4),
-                scales=ys[:, c : c + CH],
-                in_=yb[:, c : c + CH, :].rearrange("p m t -> p (m t)"),
+                out=yc[:, c : c + H].bitcast(FP8X4),
+                scales=ys[:, c : c + H],
+                in_=yb[:, c : c + H, :].rearrange("p m t -> p (m t)"),
             )
             nc.sync.dma_start(
-                out=out_1[0].rearrange("p m t -> p (m t)")[:, 4 * c : 4 * (c + CH)].bitcast(I32),
-                in_=yc[:, c : c + CH].bitcast(I32),
+                out=out_1[0].rearrange("p m t -> p (m t)")[:, 4 * c : 4 * (c + H)].bitcast(I32),
+                in_=yc[:, c : c + H].bitcast(I32),
             )
         for q in range(4):
-            nc.sync.dma_start(
+            nc.scalar.dma_start(
                 out=out_2[0, 4 * q : 4 * q + 4, :].bitcast(I32),
                 in_=ys[32 * q : 32 * q + 4, :].bitcast(I32),
             )

@@ -1,7 +1,6 @@
 from contextlib import ExitStack
 
 import concourse.mybir as mybir
-from concourse.masks import make_identity
 
 F32 = mybir.dt.float32
 BF16 = mybir.dt.bfloat16
@@ -23,6 +22,17 @@ K = 1024
 G = 2
 H = 512
 
+ORDER = """
+T0x1 T0x0 T0d1 c0x1 T0d0 c0x0 c0d1 c0d0 q0x q0d M0g M0dg sil0 M1g th0 M0du sm0 M0u sil1 c0 T1x
+th1 d0 M1du c1x a0 T1d sm1 q1x T2x b0 c1d c1 M3g c2x M2g d1 dh0 sil3 M1dg sm3 M1u q2x th3 q1d
+T2d a1 sil2 T3x c3 c2d M2du b1 th2 M3dg sm2 dh1 d2 M5g c3x a3 M4g sil5 c2 M2dg sm5 q2d M3du a2
+th4 M2u d3 th5 T3d q3x sil4 D0 c5 sm4 M3u b2 cD0 M4dg c4 M7g qD0 M5dg b3 dh2 sil7 M4u a4 c3d
+M5du dh3 a5 th7 M6g b4 sm7 M5u q3d sil6 d5 M4du sm6 M6du c7 th6 d4 D1 M6dg c6 cD1 M7du b5 dh4
+M6u a6 Y01 dh5 d6 M7dg b6 cy01 Y00 qD1 M7u a7 dh6 cy00 d7 D2 Y10 cD2 b7 D30 qD2 cy10 Y11 dh7
+cD30 Y21 cy11 qD30 i00 D31 Y20 cD31 cy21 qD31 Y31a i01 Y30a cy20 Y31b Y30b cy31 cy30 i2c i2b i2a
+qy1 qy0
+"""
+
 
 def tile_swigluforwardtangentjvp_x2_kernel(
     tc, x, dx, wg_words, wg_scales, wu_words, wu_scales, wd_words, wd_scales, out_0, out_1, out_2
@@ -40,8 +50,10 @@ def tile_swigluforwardtangentjvp_x2_kernel(
         for n in ("wg", "wu", "wd"):
             planes[n] = keep.tile([P, G, K], U8, name="plane_" + n, align_bytes=64)
             nc.vector.memset(planes[n][:].rearrange("p g n -> p (g n)").bitcast(I32), 0)
+        diag = keep.tile([P, P], F32, name="diag")
+        nc.gpsimd.iota(diag[:], pattern=[[1, P]], base=0, channel_multiplier=-1, allow_small_or_imprecise_dtypes=True)
         ident = keep.tile([P, P], F32, name="ident")
-        make_identity(nc, ident[:])
+        nc.vector.tensor_scalar(out=ident[:], in0=diag[:], scalar1=0.0, scalar2=None, op0=mybir.AluOpType.is_equal)
 
         xin = {}
 
@@ -68,11 +80,11 @@ def tile_swigluforwardtangentjvp_x2_kernel(
                     in_=src[:, 4 * q : 4 * q + 4, :].rearrange("g q n -> q g n").bitcast(I32),
                 )
 
-        load_s("wg", wg_scales, nc.scalar)
         load_x(0, 1)
+        load_s("wg", wg_scales, nc.scalar)
         load_w("wg", wg_words, 0)
         load_w("wu", wu_words, 0)
-        load_s("wu", wu_scales, nc.sync)
+        load_s("wu", wu_scales, nc.gpsimd)
         load_w("wg", wg_words, 1)
         load_w("wu", wu_words, 1)
         load_x(1, 1)
@@ -95,7 +107,7 @@ def tile_swigluforwardtangentjvp_x2_kernel(
                 nc.vector.tensor_copy(out=out, in_=in_)
 
         def x_alloc(t):
-            raw["x", t] = work.tile([P, 2, G, P * 4], BF16, name="xgrp", bufs=2, align_bytes=64)
+            raw["x", t] = work.tile([P, 2, G, P * 4], BF16, name="xgrp", bufs=4, align_bytes=64)
             codes["x", t] = keep.tile([P, 2, G, P], U32, name="cx%d" % t, align_bytes=64)
             scales["x", t] = keep.tile([P, 2, G, P], U8, name="sx%d" % t, align_bytes=64)
 
@@ -164,39 +176,42 @@ def tile_swigluforwardtangentjvp_x2_kernel(
             ew[name, i] = work.tile(list(shape), dt, name=name, bufs=bufs, align_bytes=64)
             return ew[name, i]
 
-        def act(i):
-            g = bank["g", i]
-            nc.scalar.activation(out=tile("sil", i, bufs=3)[:], in_=g[:], func=ACT.Silu)
-            nc.scalar.activation(out=tile("th", i, bufs=3)[:], in_=g[:], func=ACT.Tanh, scale=0.5)
-            nc.scalar.activation(out=tile("sm", i, bufs=3)[:], in_=ew["sil", i][:], func=ACT.Copy, scale=0.5, bias=-0.5)
+        def sil(i):
+            nc.scalar.activation(out=tile("sil", i, bufs=8)[:], in_=bank["g", i][:], func=ACT.Silu)
+
+        def th(i):
+            nc.scalar.activation(out=tile("th", i, bufs=6)[:], in_=bank["g", i][:], func=ACT.Tanh, scale=0.5)
+
+        def sm(i):
+            nc.scalar.activation(out=tile("sm", i, bufs=6)[:], in_=ew["sil", i][:], func=ACT.Copy, scale=0.5, bias=-0.5)
 
         def v_c(i):
             nc.vector.scalar_tensor_tensor(
-                out=tile("c", i)[:], in0=ew["th", i][:], scalar=1.0, in1=ew["sm", i][:], op0=SUB, op1=MUL
+                out=tile("c", i, bufs=4)[:], in0=ew["th", i][:], scalar=1.0, in1=ew["sm", i][:], op0=SUB, op1=MUL
             )
 
         def v_a(i):
             nc.vector.scalar_tensor_tensor(
-                out=tile("a", i)[:], in0=ew["c", i][:], scalar=1.0, in1=bank["dg", i][:], op0=SUB, op1=MUL
+                out=tile("a", i, bufs=4)[:], in0=ew["c", i][:], scalar=1.0, in1=bank["dg", i][:], op0=SUB, op1=MUL
             )
 
         W = (P, 2, P, 2)
 
         def v_d(i):
             nc.vector.tensor_tensor(
-                out=tile("d", i, shape=W)[:], in0=perm(ew["sil", i][:]), in1=perm(bank["du", i][:]), op=MUL
+                out=tile("d", i, shape=W, bufs=6)[:], in0=perm(ew["sil", i][:]), in1=perm(bank["du", i][:]), op=MUL
             )
 
         def v_b(i):
             nc.vector.tensor_tensor(
-                out=tile("b", i, shape=W)[:], in0=perm(ew["a", i][:]), in1=perm(bank["u", i][:]), op=MUL
+                out=tile("b", i, shape=W, bufs=6)[:], in0=perm(ew["a", i][:]), in1=perm(bank["u", i][:]), op=MUL
             )
 
         def dh(i, eng):
-            eng.tensor_tensor(out=tile("dh", i, BF16, W, 4)[:], in0=ew["d", i][:], in1=ew["b", i][:], op=SUB)
+            eng.tensor_tensor(out=tile("dh", i, BF16, W, 8)[:], in0=ew["d", i][:], in1=ew["b", i][:], op=SUB)
 
         def d_alloc(t):
-            raw["h", t] = work.tile([P, G, P * 4], BF16, name="hgrp", bufs=2, align_bytes=64)
+            raw["h", t] = work.tile([P, G, P * 4], BF16, name="hgrp", bufs=4, align_bytes=64)
             codes["h", t] = keep.tile([P, G, P], U32, name="ch%d" % t, align_bytes=64)
             scales["h", t] = keep.tile([P, G, P], U8, name="sh%d" % t, align_bytes=64)
 
@@ -262,107 +277,63 @@ def tile_swigluforwardtangentjvp_x2_kernel(
         def inter(t, lo, hi, eng):
             copy(eng, yb[:, lo:hi, t : t + 2], y[:, t : t + 2, lo:hi].rearrange("p t m -> p m t"))
 
-
         def one(h):
             return slice(h, h + 1)
 
-        def x_all(t):
+        for t in range(4):
             x_alloc(t)
-            x_full(t, 0, "S", "aux", 2)
-            x_full(t, 1, "S", "aux", 2)
+            d_alloc(t)
+        full = {}
 
-        def s2_all(t):
-            for m in range(2):
-                s2(t, m)
-                y_copy(t, m, "S")
-            y_store(t)
-
-        def step(i, before_dg=(), after_u=(), after_c=(), after_b=()):
-            if i > 0:
-                s1(i, "du")
-                if i + 1 < 8:
-                    s1(i + 1, "g")
-                    act(i + 1)
-                for f in before_dg:
-                    f()
-                s1(i, "dg")
-                s1(i, "u")
-            for f in after_u:
-                f()
-            v_c(i)
-            for f in after_c:
-                f()
-            if i > 0:
-                v_b(i - 1)
-                dh(i - 1, nc.gpsimd)
-            for f in after_b:
-                f()
-            v_d(i)
-            v_a(i)
-
-        x_alloc(0)
-        for j in range(2):
+        def x_full_pe(t, j):
+            full["x", t, j] = psum.tile([P, 4, P], F32, name="aux", bufs=2)
             for g in range(G):
-                x_half_pe(0, j, g)
-        x_half_copy(0, 0, 0, "S")
-        x_half_copy(0, 0, 1, "V")
-        x_half_copy(0, 1, 0, "S")
-        x_quant(0, one(0))
-        x_half_copy(0, 1, 1, "V")
-        x_quant(0, one(1))
-        s1(0, "g")
-        act(0)
-        s1(0, "dg")
-        s1(0, "du")
-        s1(0, "u")
-        x_all(1)
-        v_d(0)
-        v_c(0)
-        x_quant(1, one(0))
-        v_a(0)
-        x_quant(1, one(1))
-        s1(1, "g")
-        act(1)
-        x_all(2)
-        step(1, after_c=(lambda: x_quant(2, one(0)),), after_b=())
-        x_quant(2, one(1))
-        step(2, after_u=(lambda: x_all(3),))
-        step(3, before_dg=(lambda: d_full(0, "S"),), after_c=(lambda: x_quant(3, BOTH),))
-        step(4)
-        step(5, before_dg=(lambda: d_full(1, "S"),), after_c=(lambda: d_quant(0, BOTH),))
-        s2_all(0)
-        step(6, after_c=(lambda: d_quant(1, BOTH),))
-        step(7)
-        d_full(2, "S")
-        v_b(7)
-        s2_all(1)
-        d_alloc(3)
-        d_half(3, 0, "S")
-        d_quant(2, BOTH)
-        dh(7, nc.vector)
-        s2(2, 0)
-        inter(0, 0, H, "V")
-        d_quant(3, one(0))
-        d_half(3, 1, "S")
-        y_copy(2, 0, "S")
-        s2(2, 1)
-        d_quant(3, one(1))
-        inter(0, H, K, "V")
-        y_copy(2, 1, "S")
-        y_store(2)
-        for m in range(2):
-            bank["y", 3, m] = psum.tile([P, H], F32, name="s1", bufs=6)
-        for g in range(G):
-            for m in range(2):
-                s2_mm(3, m, g)
-        y_copy(3, 0, "S")
-        y_copy(3, 1, "V")
-        y_store(3, 0, H)
-        y_store(3, H, K)
-        inter(2, 640, K, "S")
-        inter(2, 0, 384, "V")
-        inter(2, 384, 640, "V")
-        for c in range(0, K, H):
+                x_pe(t, j, g, full["x", t, j], 2 * g)
+
+        def x_full_copy(t, j):
+            nc.scalar.copy(
+                out=raw["x", t][:, j, :, :].rearrange("p g n -> p (g n)").bitcast(F32).rearrange("p (g r u) -> p g r u", g=G, u=2),
+                in_=full["x", t, j][:].rearrange("p (g u) r -> p g r u", g=G),
+            )
+
+        def d_full_pe(t):
+            full["h", t] = psum.tile([P, 4, P], F32, name="aux", bufs=2)
+            for h in range(2):
+                d_pe(t, h, full["h", t], 2 * h)
+
+        def d_full_copy(t):
+            nc.scalar.copy(
+                out=raw["h", t][:].rearrange("p g n -> p (g n)").bitcast(F32).rearrange("p (g r u) -> p g r u", g=G, u=2),
+                in_=full["h", t][:].rearrange("p (g u) r -> p g r u", g=G),
+            )
+
+        def d_half_pe(h):
+            full["h", 3, h] = psum.tile([P, 2, P], F32, name="s1", bufs=6)
+            d_pe(3, h, full["h", 3, h], 0)
+
+        def d_half_copy(h):
+            nc.scalar.copy(
+                out=raw["h", 3][:, h, :].bitcast(F32).rearrange("p (r u) -> p r u", u=2),
+                in_=full["h", 3, h][:].rearrange("p u r -> p r u"),
+            )
+
+        def y_last(m, g):
+            if g == 0:
+                bank["y", 3, m] = psum.tile([P, H], F32, name="s1", bufs=6)
+            s2_mm(3, m, g)
+
+        done = set()
+
+        def y_out(t, m):
+            y_copy(t, m, "V" if (t, m) == (3, 1) else "S")
+            done.add((t, m))
+            if t == 3:
+                y_store(t, m * H, (m + 1) * H)
+            elif (t, 1 - m) in done:
+                y_store(t)
+
+        def planes_out(m):
+            c = m * H
             nc.vector.quantize_mx(
                 out=yc[:, c : c + H].bitcast(FP8X4),
                 scales=ys[:, c : c + H],
@@ -372,6 +343,46 @@ def tile_swigluforwardtangentjvp_x2_kernel(
                 out=out_1[0].rearrange("p m t -> p (m t)")[:, 4 * c : 4 * (c + H)].bitcast(I32),
                 in_=yc[:, c : c + H].bitcast(I32),
             )
+
+        ops = {}
+        for j in range(2):
+            n = "xd"[j]
+            for g in range(G):
+                ops["T0%s%d" % (n, g)] = (x_half_pe, 0, j, g)
+                ops["c0%s%d" % (n, g)] = (x_half_copy, 0, j, g, "SV"[g])
+            for t in range(1, 4):
+                ops["T%d%s" % (t, n)] = (x_full_pe, t, j)
+                ops["c%d%s" % (t, n)] = (x_full_copy, t, j)
+            for t in range(4):
+                ops["q%d%s" % (t, n)] = (x_quant, t, one(j))
+        for i in range(8):
+            for w in ("g", "dg", "u", "du"):
+                ops["M%d%s" % (i, w)] = (s1, i, w)
+            for n, f in (("sil", sil), ("th", th), ("sm", sm), ("c", v_c), ("a", v_a), ("d", v_d), ("b", v_b)):
+                ops["%s%d" % (n, i)] = (f, i)
+            ops["dh%d" % i] = (dh, i, nc.vector if i == 7 else nc.gpsimd)
+        for t in range(3):
+            ops["D%d" % t] = (d_full_pe, t)
+            ops["cD%d" % t] = (d_full_copy, t)
+            ops["qD%d" % t] = (d_quant, t, BOTH)
+        for h in range(2):
+            ops["D3%d" % h] = (d_half_pe, h)
+            ops["cD3%d" % h] = (d_half_copy, h)
+            ops["qD3%d" % h] = (d_quant, 3, one(h))
+            for t in range(4):
+                ops["cy%d%d" % (t, h)] = (y_out, t, h)
+                if t < 3:
+                    ops["Y%d%d" % (t, h)] = (s2, t, h)
+            ops["Y3%da" % h] = (y_last, h, 0)
+            ops["Y3%db" % h] = (y_last, h, 1)
+            ops["i0%d" % h] = (inter, 0, h * H, (h + 1) * H, "V")
+            ops["qy%d" % h] = (planes_out, h)
+        ops["i2a"] = (inter, 2, 0, 384, "V")
+        ops["i2b"] = (inter, 2, 384, 640, "V")
+        ops["i2c"] = (inter, 2, 640, K, "S")
+        for token in ORDER.split():
+            op = ops[token]
+            op[0](*op[1:])
         for q in range(4):
             nc.scalar.dma_start(
                 out=out_2[0, 4 * q : 4 * q + 4, :].bitcast(I32),

from contextlib import ExitStack

import concourse.mybir as mybir

F32 = mybir.dt.float32
BF16 = mybir.dt.bfloat16
U32 = mybir.dt.uint32
I32 = mybir.dt.int32
U8 = mybir.dt.uint8
FP8X4 = mybir.dt.float8_e4m3fn_x4
FP4X4 = mybir.dt.float4_e2m1fn_x4
ADD = mybir.AluOpType.add
SUB = mybir.AluOpType.subtract
MUL = mybir.AluOpType.mult
ACT = mybir.ActivationFunctionType

FLOPS = 5 * 2 * 512 * 1024 * 1024

P = 128
T = 4
K = 1024
G = 2
H = 512

ORDER = """
T0x1 T0x0 T0d1 c0x1 T0d0 c0x0 c0d1 c0d0 q0x q0d M0g M0dg sil0 M1g th0 M0du sm0 M0u sil1 c0 T1x
th1 d0 M1du c1x a0 T1d sm1 q1x T2x b0 c1d c1 M3g c2x M2g d1 dh0 sil3 M1dg sm3 M1u q2x th3 q1d
T2d a1 sil2 T3x c3 c2d M2du b1 th2 M3dg sm2 dh1 d2 M5g c3x a3 M4g sil5 c2 M2dg sm5 q2d M3du a2
th4 M2u d3 th5 T3d q3x sil4 D0 c5 sm4 M3u b2 cD0 M4dg c4 M7g qD0 M5dg b3 dh2 sil7 M4u a4 c3d
M5du dh3 a5 th7 M6g b4 sm7 M5u q3d sil6 d5 M4du sm6 M6du c7 th6 d4 D1 M6dg c6 cD1 M7du b5 dh4
M6u a6 Y01 dh5 d6 M7dg b6 cy01 Y00 qD1 M7u a7 dh6 cy00 d7 D2 Y10 cD2 b7 D30 qD2 cy10 Y11 dh7
cD30 Y21 cy11 qD30 i00 D31 Y20 cD31 cy21 qD31 Y31a i01 Y30a cy20 Y31b Y30b cy31 cy30 i2c i2b i2a
qy1 qy0
"""


def tile_swigluforwardtangentjvp_x2_kernel(
    tc, x, dx, wg_words, wg_scales, wu_words, wu_scales, wd_words, wd_scales, out_0, out_1, out_2
):
    nc = tc.nc
    with ExitStack() as ctx:
        keep = ctx.enter_context(tc.tile_pool(name="keep", bufs=1))
        work = ctx.enter_context(tc.tile_pool(name="work", bufs=2))
        psum = ctx.enter_context(tc.psum_pool(name="psum", bufs=1))
        ctx.enter_context(tc.manual_schedule())

        y_rows = out_0.rearrange("(p t) m -> p t m", t=T)

        planes = {}
        for n in ("wg", "wu", "wd"):
            planes[n] = keep.tile([P, G, K], U8, name="plane_" + n, align_bytes=64)
            nc.vector.memset(planes[n][:].rearrange("p g n -> p (g n)").bitcast(I32), 0)
        diag = keep.tile([P, P], F32, name="diag")
        nc.gpsimd.iota(diag[:], pattern=[[1, P]], base=0, channel_multiplier=-1, allow_small_or_imprecise_dtypes=True)
        ident = keep.tile([P, P], F32, name="ident")
        nc.vector.tensor_scalar(out=ident[:], in0=diag[:], scalar1=0.0, scalar2=None, op0=mybir.AluOpType.is_equal)

        xin = {}

        def load_x(t, n):
            for nm, src in (("x", x), ("d", dx)):
                b = keep.tile([P, n, K], BF16, name="in_%s%d" % (nm, t), align_bytes=64)
                nc.sync.dma_start(out=b[:], in_=src.rearrange("(p t) k -> p t k", t=T)[:, t : t + n, :])
                for s in range(n):
                    xin[nm, t + s] = b[:, s, :]

        words = {}

        def load_w(n, src, half):
            words[n, half] = keep.tile([P, G, K], U8, name="w_%s%d" % (n, half), align_bytes=64)
            nc.sync.dma_start(
                out=words[n, half][:].bitcast(I32),
                in_=src.rearrange("g p b -> p g b")[:, :, half * K : (half + 1) * K].bitcast(I32),
            )

        def load_s(n, src, eng):
            for q in range(4):
                eng.dma_start(
                    out=planes[n][32 * q : 32 * q + 4, :, :].bitcast(I32),
                    in_=src[:, 4 * q : 4 * q + 4, :].rearrange("g q n -> q g n").bitcast(I32),
                )

        load_x(0, 1)
        load_s("wg", wg_scales, nc.scalar)
        load_w("wg", wg_words, 0)
        load_w("wu", wu_words, 0)
        load_s("wu", wu_scales, nc.gpsimd)
        load_w("wg", wg_words, 1)
        load_w("wu", wu_words, 1)
        load_x(1, 1)
        load_x(2, 2)
        load_s("wd", wd_scales, nc.sync)
        load_w("wd", wd_words, 0)
        load_w("wd", wd_words, 1)
        warm = keep.tile([P, 1], F32, name="warm")
        nc.vector.memset(warm[:], 0.0)
        nc.scalar.activation(out=warm[:], in_=warm[:], func=ACT.Silu)

        codes = {}
        scales = {}
        raw = {}

        def copy(eng, out, in_):
            if eng == "S":
                nc.scalar.copy(out=out, in_=in_)
            else:
                nc.vector.tensor_copy(out=out, in_=in_)

        def x_alloc(t):
            raw["x", t] = work.tile([P, 2, G, P * 4], BF16, name="xgrp", bufs=4, align_bytes=64)
            codes["x", t] = keep.tile([P, 2, G, P], U32, name="cx%d" % t, align_bytes=64)
            scales["x", t] = keep.tile([P, 2, G, P], U8, name="sx%d" % t, align_bytes=64)

        def x_pe(t, j, g, b, s):
            w = xin["xd"[j], t].bitcast(F32)
            for u in range(2):
                nc.tensor.transpose(b[:, s + u, :], w[:, 256 * g + u : 256 * (g + 1) : 2], ident[:])

        half = {}

        def x_half_pe(t, j, g):
            half[t, j, g] = psum.tile([P, 2, P], F32, name="s1", bufs=6)
            x_pe(t, j, g, half[t, j, g], 0)

        def x_half_copy(t, j, g, eng):
            copy(
                eng,
                raw["x", t][:, j, g, :].bitcast(F32).rearrange("p (r u) -> p r u", u=2),
                half[t, j, g][:].rearrange("p u r -> p r u"),
            )

        def x_full(t, j, eng, tag, bufs):
            b = psum.tile([P, 4, P], F32, name=tag, bufs=bufs)
            for g in range(G):
                x_pe(t, j, g, b, 2 * g)
            copy(
                eng,
                raw["x", t][:, j, :, :].rearrange("p g n -> p (g n)").bitcast(F32).rearrange("p (g r u) -> p g r u", g=G, u=2),
                b[:].rearrange("p (g u) r -> p g r u", g=G),
            )

        def x_quant(t, sel):
            nc.vector.quantize_mx(
                out=codes["x", t][:, sel].rearrange("p j g r -> p (j g r)").bitcast(FP8X4),
                scales=scales["x", t][:, sel].rearrange("p j g r -> p (j g r)"),
                in_=raw["x", t][:, sel].rearrange("p j g n -> p (j g n)"),
            )

        BOTH = slice(0, 2)

        bank = {}
        PROD = {"g": (0, "wg"), "dg": (1, "wg"), "u": (0, "wu"), "du": (1, "wu")}

        def s1(i, which):
            t, h = divmod(i, 2)
            j, wn = PROD[which]
            b = psum.tile([P, H], F32, name="s1", bufs=6)
            bank[which, i] = b
            for g in range(G):
                nc.tensor.matmul_mx(
                    out=b[:],
                    lhsT=codes["x", t][:, j, g, :].bitcast(FP8X4),
                    lhsT_scale=scales["x", t][:, j, g, :],
                    rhs=words[wn, h][:, g, :].bitcast(FP4X4),
                    rhs_scale=planes[wn][:, g, h * H : (h + 1) * H],
                    start=(g == 0),
                    stop=(g == G - 1),
                )

        ew = {}

        def perm(ap):
            return ap.rearrange("p (q u e) -> p u q e", u=2, e=2)

        def tile(name, i, dt=F32, shape=(P, H), bufs=2):
            ew[name, i] = work.tile(list(shape), dt, name=name, bufs=bufs, align_bytes=64)
            return ew[name, i]

        def sil(i):
            nc.scalar.activation(out=tile("sil", i, bufs=8)[:], in_=bank["g", i][:], func=ACT.Silu)

        def th(i):
            nc.scalar.activation(out=tile("th", i, bufs=6)[:], in_=bank["g", i][:], func=ACT.Tanh, scale=0.5)

        def sm(i):
            nc.scalar.activation(out=tile("sm", i, bufs=6)[:], in_=ew["sil", i][:], func=ACT.Copy, scale=0.5, bias=-0.5)

        def v_c(i):
            nc.vector.scalar_tensor_tensor(
                out=tile("c", i, bufs=4)[:], in0=ew["th", i][:], scalar=1.0, in1=ew["sm", i][:], op0=SUB, op1=MUL
            )

        def v_a(i):
            nc.vector.scalar_tensor_tensor(
                out=tile("a", i, bufs=4)[:], in0=ew["c", i][:], scalar=1.0, in1=bank["dg", i][:], op0=SUB, op1=MUL
            )

        W = (P, 2, P, 2)

        def v_d(i):
            nc.vector.tensor_tensor(
                out=tile("d", i, shape=W, bufs=6)[:], in0=perm(ew["sil", i][:]), in1=perm(bank["du", i][:]), op=MUL
            )

        def v_b(i):
            nc.vector.tensor_tensor(
                out=tile("b", i, shape=W, bufs=6)[:], in0=perm(ew["a", i][:]), in1=perm(bank["u", i][:]), op=MUL
            )

        def dh(i, eng):
            eng.tensor_tensor(out=tile("dh", i, BF16, W, 8)[:], in0=ew["d", i][:], in1=ew["b", i][:], op=SUB)

        def d_alloc(t):
            raw["h", t] = work.tile([P, G, P * 4], BF16, name="hgrp", bufs=4, align_bytes=64)
            codes["h", t] = keep.tile([P, G, P], U32, name="ch%d" % t, align_bytes=64)
            scales["h", t] = keep.tile([P, G, P], U8, name="sh%d" % t, align_bytes=64)

        def d_pe(t, h, b, s):
            w = ew["dh", 2 * t + h][:].rearrange("p u q e -> p (u q e)").bitcast(F32)
            for u in range(2):
                nc.tensor.transpose(b[:, s + u, :], w[:, P * u : P * (u + 1)], ident[:])

        def d_full(t, eng):
            d_alloc(t)
            b = psum.tile([P, 4, P], F32, name="aux", bufs=2)
            for h in range(2):
                d_pe(t, h, b, 2 * h)
            copy(
                eng,
                raw["h", t][:].rearrange("p g n -> p (g n)").bitcast(F32).rearrange("p (g r u) -> p g r u", g=G, u=2),
                b[:].rearrange("p (g u) r -> p g r u", g=G),
            )

        def d_half(t, h, eng):
            b = psum.tile([P, 2, P], F32, name="s1", bufs=6)
            d_pe(t, h, b, 0)
            copy(
                eng,
                raw["h", t][:, h, :].bitcast(F32).rearrange("p (r u) -> p r u", u=2),
                b[:].rearrange("p u r -> p r u"),
            )

        def d_quant(t, sel):
            nc.vector.quantize_mx(
                out=codes["h", t][:, sel].rearrange("p g r -> p (g r)").bitcast(FP8X4),
                scales=scales["h", t][:, sel].rearrange("p g r -> p (g r)"),
                in_=raw["h", t][:, sel].rearrange("p g n -> p (g n)"),
            )

        y = keep.tile([P, T, K], F32, name="y", align_bytes=64)
        yb = keep.tile([P, K, T], BF16, name="yb", align_bytes=64)
        yc = keep.tile([P, K], U32, name="yc", align_bytes=64)
        ys = keep.tile([P, K], U8, name="ys", align_bytes=64)

        def s2_mm(t, m, g):
            nc.tensor.matmul_mx(
                out=bank["y", t, m][:],
                lhsT=codes["h", t][:, g, :].bitcast(FP8X4),
                lhsT_scale=scales["h", t][:, g, :],
                rhs=words["wd", m][:, g, :].bitcast(FP4X4),
                rhs_scale=planes["wd"][:, g, m * H : (m + 1) * H],
                start=(g == 0),
                stop=(g == G - 1),
            )

        def s2(t, m):
            bank["y", t, m] = psum.tile([P, H], F32, name="aux", bufs=2)
            for g in range(G):
                s2_mm(t, m, g)

        def y_copy(t, m, eng):
            copy(eng, y[:, t, m * H : (m + 1) * H], bank["y", t, m][:])

        def y_store(t, lo=0, hi=K):
            nc.sync.dma_start(out=y_rows[:, t, lo:hi], in_=y[:, t, lo:hi])

        def inter(t, lo, hi, eng):
            copy(eng, yb[:, lo:hi, t : t + 2], y[:, t : t + 2, lo:hi].rearrange("p t m -> p m t"))

        def one(h):
            return slice(h, h + 1)

        for t in range(4):
            x_alloc(t)
            d_alloc(t)
        full = {}

        def x_full_pe(t, j):
            full["x", t, j] = psum.tile([P, 4, P], F32, name="aux", bufs=2)
            for g in range(G):
                x_pe(t, j, g, full["x", t, j], 2 * g)

        def x_full_copy(t, j):
            nc.scalar.copy(
                out=raw["x", t][:, j, :, :].rearrange("p g n -> p (g n)").bitcast(F32).rearrange("p (g r u) -> p g r u", g=G, u=2),
                in_=full["x", t, j][:].rearrange("p (g u) r -> p g r u", g=G),
            )

        def d_full_pe(t):
            full["h", t] = psum.tile([P, 4, P], F32, name="aux", bufs=2)
            for h in range(2):
                d_pe(t, h, full["h", t], 2 * h)

        def d_full_copy(t):
            nc.scalar.copy(
                out=raw["h", t][:].rearrange("p g n -> p (g n)").bitcast(F32).rearrange("p (g r u) -> p g r u", g=G, u=2),
                in_=full["h", t][:].rearrange("p (g u) r -> p g r u", g=G),
            )

        def d_half_pe(h):
            full["h", 3, h] = psum.tile([P, 2, P], F32, name="s1", bufs=6)
            d_pe(3, h, full["h", 3, h], 0)

        def d_half_copy(h):
            nc.scalar.copy(
                out=raw["h", 3][:, h, :].bitcast(F32).rearrange("p (r u) -> p r u", u=2),
                in_=full["h", 3, h][:].rearrange("p u r -> p r u"),
            )

        def y_last(m, g):
            if g == 0:
                bank["y", 3, m] = psum.tile([P, H], F32, name="s1", bufs=6)
            s2_mm(3, m, g)

        done = set()

        def y_out(t, m):
            y_copy(t, m, "V" if (t, m) == (3, 1) else "S")
            done.add((t, m))
            if t == 3:
                y_store(t, m * H, (m + 1) * H)
            elif (t, 1 - m) in done:
                y_store(t)

        def planes_out(m):
            c = m * H
            nc.vector.quantize_mx(
                out=yc[:, c : c + H].bitcast(FP8X4),
                scales=ys[:, c : c + H],
                in_=yb[:, c : c + H, :].rearrange("p m t -> p (m t)"),
            )
            nc.sync.dma_start(
                out=out_1[0].rearrange("p m t -> p (m t)")[:, 4 * c : 4 * (c + H)].bitcast(I32),
                in_=yc[:, c : c + H].bitcast(I32),
            )

        ops = {}
        for j in range(2):
            n = "xd"[j]
            for g in range(G):
                ops["T0%s%d" % (n, g)] = (x_half_pe, 0, j, g)
                ops["c0%s%d" % (n, g)] = (x_half_copy, 0, j, g, "SV"[g])
            for t in range(1, 4):
                ops["T%d%s" % (t, n)] = (x_full_pe, t, j)
                ops["c%d%s" % (t, n)] = (x_full_copy, t, j)
            for t in range(4):
                ops["q%d%s" % (t, n)] = (x_quant, t, one(j))
        for i in range(8):
            for w in ("g", "dg", "u", "du"):
                ops["M%d%s" % (i, w)] = (s1, i, w)
            for n, f in (("sil", sil), ("th", th), ("sm", sm), ("c", v_c), ("a", v_a), ("d", v_d), ("b", v_b)):
                ops["%s%d" % (n, i)] = (f, i)
            ops["dh%d" % i] = (dh, i, nc.vector if i == 7 else nc.gpsimd)
        for t in range(3):
            ops["D%d" % t] = (d_full_pe, t)
            ops["cD%d" % t] = (d_full_copy, t)
            ops["qD%d" % t] = (d_quant, t, BOTH)
        for h in range(2):
            ops["D3%d" % h] = (d_half_pe, h)
            ops["cD3%d" % h] = (d_half_copy, h)
            ops["qD3%d" % h] = (d_quant, 3, one(h))
            for t in range(4):
                ops["cy%d%d" % (t, h)] = (y_out, t, h)
                if t < 3:
                    ops["Y%d%d" % (t, h)] = (s2, t, h)
            ops["Y3%da" % h] = (y_last, h, 0)
            ops["Y3%db" % h] = (y_last, h, 1)
            ops["i0%d" % h] = (inter, 0, h * H, (h + 1) * H, "V")
            ops["qy%d" % h] = (planes_out, h)
        ops["i2a"] = (inter, 2, 0, 384, "V")
        ops["i2b"] = (inter, 2, 384, 640, "V")
        ops["i2c"] = (inter, 2, 640, K, "S")
        for token in ORDER.split():
            op = ops[token]
            op[0](*op[1:])
        for q in range(4):
            nc.scalar.dma_start(
                out=out_2[0, 4 * q : 4 * q + 4, :].bitcast(I32),
                in_=ys[32 * q : 32 * q + 4, :].bitcast(I32),
            )
